import numpy as np
import ml_dtypes


def mxq(x, axis, fmt="e4m3"):
    dtype, down = {"e4m3": (ml_dtypes.float8_e4m3fn, 7), "e5m2": (ml_dtypes.float8_e5m2, 14)}[fmt]
    v = np.moveaxis(np.asarray(x, np.float32).astype(ml_dtypes.bfloat16).astype(np.float64), axis, -1)
    blocks = v.reshape(v.shape[:-1] + (-1, 32))
    amax = np.abs(blocks).max(-1, keepdims=True)
    byte = np.maximum(np.where(amax > 0, np.frexp(amax)[1] - 1 + 127, 0) - down, 1)
    scale = np.exp2(byte - 127.0)
    codes = (blocks / scale).astype(np.float32).astype(dtype).astype(np.float64)
    return np.moveaxis((codes * scale).reshape(v.shape), -1, axis)


WIDE = False


def mx_kscale(k):
    if not WIDE:
        return np.ones(k)
    levels = np.array([10, -10, 5, -5, 0])
    if k % 512:
        return np.exp2(np.random.permutation(np.resize(levels, k // 32))).repeat(32)
    a = np.empty((k // 512, 16))
    for p in range(k // 512):
        a[p, :8] = np.random.permutation(np.resize(levels, 8))
        for g in range(8):
            far = levels[np.abs(levels - a[p, g]) >= 10]
            a[p, g + 8] = far[np.random.randint(len(far))]
    return np.exp2(a.ravel()).repeat(32)


def f64(x):
    return np.asarray(x).astype(np.float64)


def striped8(idx):
    return np.concatenate([v.reshape(-1, 16).T for v in idx]).astype(np.uint16)


def unstriped8(offs):
    return np.stack([offs[16 * g:16 * g + 16].T.reshape(-1) for g in range(8)]).astype(np.int64)


E2M1 = np.array([0.0, 0.5, 1.0, 1.5, 2.0, 3.0, 4.0, 6.0, -0.0, -0.5, -1.0, -1.5, -2.0, -3.0, -4.0, -6.0])


def pack_weight(w, fmt):
    k, n = w.shape
    w = f64(np.asarray(w, np.float32).astype(ml_dtypes.bfloat16)).reshape(k // 32, 32, n)
    amax = np.abs(w).max(1)
    if fmt == "e4m3":
        byte = np.frexp(amax)[1] - 1 + 127 - 7
    else:
        mant, ex = np.frexp(amax / 6.0)
        byte = np.where(mant > 0.5, ex, ex - 1) + 127
    byte = np.clip(np.where(amax > 0, byte, 1), 1, 254)
    scaled = (w * np.exp2(127.0 - byte)[:, None, :]).reshape(k, n).astype(np.float32)
    by_word = np.ascontiguousarray(scaled.reshape(k // 512, 128, 4, n).transpose(0, 1, 3, 2))
    if fmt == "e4m3":
        words = by_word.astype(ml_dtypes.float8_e4m3fn).view(np.uint8)
    else:
        c = by_word.astype(ml_dtypes.float4_e2m1fn).view(np.uint8) & 0xF
        words = (c[..., 0::2] | (c[..., 1::2] << 4)).reshape(k // 512, 128, 2 * n)
    return np.ascontiguousarray(words), np.ascontiguousarray(byte.astype(np.uint8).reshape(k // 512, 16, n))


def unpack_weight(words, scales, fmt):
    g, _, n = scales.shape
    words = np.ascontiguousarray(words).reshape(g, 128, n, -1)
    if fmt == "e4m3":
        vals = words.view(ml_dtypes.float8_e4m3fn).astype(np.float64)
    else:
        nib = np.empty((g, 128, n, 4), np.uint8)
        nib[..., 0::2] = words & 0xF
        nib[..., 1::2] = words >> 4
        vals = E2M1[nib]
    vals = vals * np.repeat(np.exp2(scales.astype(np.float64) - 127.0), 8, axis=1)[..., None]
    return vals.transpose(0, 1, 3, 2).reshape(g * 512, n)


K, M, T, S = 1024, 1024, 1024, 512


def setup_inputs():
    n = np.random.standard_normal
    s = mx_kscale(K)[:, None]
    p_w = pack_weight(n((K, M)) / np.sqrt(K) / s, "e2m1")
    return {
        "xT": (n((K, T)) * s).astype(np.float32),
        "w_words": p_w[0],
        "w_scales": p_w[1],
        "wgt": np.repeat(np.random.uniform(0.5, 2.0, (8, S)), 16, axis=0).astype(np.float32),
        "wgo": np.repeat(np.random.uniform(0.5, 2.0, (8, S)), 16, axis=0).astype(np.float32),
        "offs": striped8(np.stack([np.random.permutation(T)[:S] for _ in range(8)])),
        "offs2": striped8(np.stack([np.random.permutation(T)[:S] for _ in range(8)])),
    }


def reference(xT, w_words, w_scales, wgt, wgo, offs, offs2):
    idx = unstriped8(offs)
    group = np.arange(K) % 512 // 64
    xg = f64(wgt)[np.arange(K) // 4 % 128] * f64(xT)[np.arange(K)[:, None], idx[group]]
    xT_ = mxq(xg, 0, "e4m3")
    w_ = unpack_weight(w_words, w_scales, "e2m1")
    y = w_.T @ xT_
    place = unstriped8(offs2)[np.arange(M) % 128 // 16]
    out = np.zeros((M, T))
    out[np.arange(M)[:, None], place] = f64(wgo)[np.arange(M) % 128] * (y)
    return out

@@ -1,0 +1,144 @@
+import concourse.mybir as mybir
+
+K, M, T, S = 1024, 1024, 1024, 512
+FLOPS = 2 * K * M * S
+
+F32 = mybir.dt.float32
+BF16 = mybir.dt.bfloat16
+I32 = mybir.dt.int32
+U32 = mybir.dt.uint32
+U16 = mybir.dt.uint16
+U8 = mybir.dt.uint8
+FP8X4 = mybir.dt.float8_e4m3fn_x4
+FP4X4 = mybir.dt.float4_e2m1fn_x4
+MULT = mybir.AluOpType.mult
+
+P = 128
+PACK = 4
+PASSES = K // (P * PACK)
+BLOCKS = M // P
+HALF = S // 2
+CHUNK = 128
+OFF_COLS = HALF // 16
+
+
+def tile_list_hboth_none_kernel(tc, xT, w_words, w_scales, wgt, wgo, offs, offs2, out):
+    nc = tc.nc
+    with tc.tile_pool(name="held", bufs=1) as held, tc.psum_pool(name="psum", bufs=1) as psum:
+        list_in = held.tile([P, S // 16], U16, name="list_in")
+        list_out = held.tile([P, S // 16], U16, name="list_out")
+        wgt_sb = held.tile([P, S], F32, name="wgt_sb")
+        wgo_sb = held.tile([P, S], F32, name="wgo_sb")
+        w_sb = held.tile([P, PASSES, 2 * M], U8, name="w_sb", align_bytes=64)
+        wsc = held.tile([P, PASSES, M], U8, name="wsc", align_bytes=64)
+        plane = [[held.tile([P, T], F32, name=f"plane{a}_{t}") for t in range(PACK)] for a in range(PASSES)]
+        picked = [[held.tile([P, PACK, HALF], F32, name=f"picked{a}_{h}") for h in range(2)] for a in range(PASSES)]
+        grouped = [[held.tile([P, HALF, PACK], BF16, name=f"grouped{a}_{h}", align_bytes=64) for h in range(2)] for a in range(PASSES)]
+        codes = [[held.tile([P, HALF], U32, name=f"codes{a}_{h}", align_bytes=64) for h in range(2)] for a in range(PASSES)]
+        xsc = [[held.tile([P, HALF], U8, name=f"xsc{a}_{h}", align_bytes=64) for h in range(2)] for a in range(PASSES)]
+        window = [held.tile([P, T], F32, name=f"window{b}") for b in range(BLOCKS)]
+        y_sb = [held.tile([P, S], F32, name=f"y{b}") for b in range(BLOCKS)]
+        bank = [psum.tile([P, S], F32, name=f"bank{b}") for b in range(BLOCKS)]
+
+        nc.gpsimd.memset(wsc[:].bitcast(I32), 0)
+        for b in range(BLOCKS):
+            nc.gpsimd.memset(window[b][:], 0.0)
+
+        rows = xT.rearrange("(a p t) n -> a t p n", p=P, t=PACK)
+        nc.sync.dma_start(list_in[:], offs)
+        nc.scalar.dma_start(wgt_sb[:, 0:HALF], wgt[:, 0:HALF])
+        nc.sync.dma_start(plane[0][0][:], rows[0, 0])
+        nc.sync.dma_start(wgt_sb[:, HALF:S], wgt[:, HALF:S])
+        for a in range(PASSES):
+            for t in range(PACK):
+                if a + t > 0:
+                    nc.sync.dma_start(plane[a][t][:], rows[a, t])
+        nc.sync.dma_start(w_sb[:].bitcast(I32), w_words.bitcast(I32).rearrange("a p n -> p a n"))
+        for q in range(4):
+            nc.sync.dma_start(
+                wsc[32 * q : 32 * q + 4].bitcast(I32),
+                w_scales.bitcast(I32)[:, 4 * q : 4 * q + 4, :].rearrange("a r n -> r a n"),
+            )
+        nc.sync.dma_start(list_out[:], offs2)
+        nc.sync.dma_start(wgo_sb[:], wgo)
+
+        def gather(a, t, h):
+            nc.vector.tensor_tensor(
+                picked[a][h][:, t, :],
+                plane[a][t][:].indirect(list_in[:, h * OFF_COLS : (h + 1) * OFF_COLS]),
+                wgt_sb[:, h * HALF : (h + 1) * HALF],
+                MULT,
+            )
+
+        def views(a, h, lo, hi):
+            return grouped[a][h][:, lo:hi, :], picked[a][h][:, :, lo:hi].rearrange("p t c -> p c t")
+
+        def interleave_scalar(a, h, lo, hi):
+            dst, src = views(a, h, lo, hi)
+            nc.scalar.copy(dst, src)
+
+        def interleave_vector(a, h, lo, hi):
+            dst, src = views(a, h, lo, hi)
+            nc.vector.tensor_copy(dst, src)
+
+        def quantize(a, h):
+            nc.vector.quantize_mx(
+                out=codes[a][h][:].bitcast(FP8X4),
+                scales=xsc[a][h][:],
+                in_=grouped[a][h][:].rearrange("p c t -> p (c t)"),
+            )
+
+        def multiply(b, h):
+            for c in range(HALF // CHUNK):
+                lo = c * CHUNK
+                for a in range(PASSES):
+                    nc.tensor.matmul_mx(
+                        out=bank[b][:, h * HALF + lo : h * HALF + lo + CHUNK],
+                        lhsT=w_sb[:, a, 2 * P * b : 2 * P * (b + 1)].bitcast(FP4X4),
+                        lhsT_scale=wsc[:, a, P * b : P * (b + 1)],
+                        rhs=codes[a][h][:, lo : lo + CHUNK].bitcast(FP8X4),
+                        rhs_scale=xsc[a][h][:, lo : lo + CHUNK],
+                        start=(a == 0),
+                        stop=(a == PASSES - 1),
+                    )
+            cols = slice(h * HALF, (h + 1) * HALF)
+            nc.scalar.copy(y_sb[b][:, cols], bank[b][:, cols])
+
+        def scatter(b, h):
+            cols = slice(h * HALF, (h + 1) * HALF)
+            nc.vector.tensor_tensor(
+                window[b][:].indirect(list_out[:, h * OFF_COLS : (h + 1) * OFF_COLS]),
+                y_sb[b][:, cols],
+                wgo_sb[:, cols],
+                MULT,
+            )
+
+        for t in range(PACK):
+            gather(0, t, 0)
+            gather(0, t, 1)
+        interleave_scalar(0, 0, 0, HALF)
+        interleave_scalar(0, 1, 0, HALF)
+        gather(1, 0, 0)
+        gather(1, 0, 1)
+        gather(1, 1, 0)
+        quantize(0, 0)
+        gather(1, 1, 1)
+        gather(1, 2, 0)
+        gather(1, 3, 0)
+        interleave_scalar(1, 0, 0, CHUNK)
+        gather(1, 2, 1)
+        gather(1, 3, 1)
+        interleave_vector(1, 0, CHUNK, HALF)
+        quantize(0, 1)
+        quantize(1, 0)
+        for b in range(BLOCKS):
+            multiply(b, 0)
+            scatter(b, 0)
+            if b == 1:
+                interleave_scalar(1, 1, 0, HALF)
+            if b == 3:
+                quantize(1, 1)
+        for b in range(BLOCKS):
+            multiply(b, 1)
+            scatter(b, 1)
+            nc.sync.dma_start(out[P * b : P * (b + 1), :], window[b][:])

@@ -42,12 +42,14 @@ def tile_list_hboth_none_kernel(tc, xT, w_words, w_scales, wgt, wgo, offs, offs2
 
         nc.gpsimd.memset(wsc[:].bitcast(I32), 0)
         for b in range(BLOCKS):
+            nc.vector.memset(window[b][:] if b < 4 else window[b][:, 0:8], 0.0)
+        for b in range(4, BLOCKS):
             nc.gpsimd.memset(window[b][:], 0.0)
 
         rows = xT.rearrange("(a p t) n -> a t p n", p=P, t=PACK)
         nc.sync.dma_start(list_in[:], offs)
-        nc.scalar.dma_start(wgt_sb[:, 0:HALF], wgt[:, 0:HALF])
         nc.sync.dma_start(plane[0][0][:], rows[0, 0])
+        nc.scalar.dma_start(wgt_sb[:, 0:HALF], wgt[:, 0:HALF])
         nc.sync.dma_start(wgt_sb[:, HALF:S], wgt[:, HALF:S])
         for a in range(PASSES):
             for t in range(PACK):
@@ -81,11 +83,11 @@ def tile_list_hboth_none_kernel(tc, xT, w_words, w_scales, wgt, wgo, offs, offs2
             dst, src = views(a, h, lo, hi)
             nc.vector.tensor_copy(dst, src)
 
-        def quantize(a, h):
+        def quantize(a, h, lo, hi):
             nc.vector.quantize_mx(
-                out=codes[a][h][:].bitcast(FP8X4),
-                scales=xsc[a][h][:],
-                in_=grouped[a][h][:].rearrange("p c t -> p (c t)"),
+                out=codes[a][h][:, lo:hi].bitcast(FP8X4),
+                scales=xsc[a][h][:, lo:hi],
+                in_=grouped[a][h][:, lo:hi, :].rearrange("p c t -> p (c t)"),
             )
 
         def multiply(b, h):
@@ -121,23 +123,24 @@ def tile_list_hboth_none_kernel(tc, xT, w_words, w_scales, wgt, wgo, offs, offs2
         gather(1, 0, 0)
         gather(1, 0, 1)
         gather(1, 1, 0)
-        quantize(0, 0)
+        quantize(0, 0, 0, HALF)
         gather(1, 1, 1)
         gather(1, 2, 0)
         gather(1, 3, 0)
         interleave_scalar(1, 0, 0, CHUNK)
         gather(1, 2, 1)
-        gather(1, 3, 1)
         interleave_vector(1, 0, CHUNK, HALF)
-        quantize(0, 1)
-        quantize(1, 0)
+        quantize(1, 0, 0, CHUNK)
+        quantize(1, 0, CHUNK, HALF)
+        gather(1, 3, 1)
+        quantize(0, 1, 0, HALF)
         for b in range(BLOCKS):
             multiply(b, 0)
             scatter(b, 0)
             if b == 1:
                 interleave_scalar(1, 1, 0, HALF)
             if b == 3:
-                quantize(1, 1)
+                quantize(1, 1, 0, HALF)
         for b in range(BLOCKS):
             multiply(b, 1)
             scatter(b, 1)

import concourse.mybir as mybir

K, M, T, S = 1024, 1024, 1024, 512
FLOPS = 2 * K * M * S

F32 = mybir.dt.float32
BF16 = mybir.dt.bfloat16
I32 = mybir.dt.int32
U32 = mybir.dt.uint32
U16 = mybir.dt.uint16
U8 = mybir.dt.uint8
FP8X4 = mybir.dt.float8_e4m3fn_x4
FP4X4 = mybir.dt.float4_e2m1fn_x4
MULT = mybir.AluOpType.mult

P = 128
PACK = 4
PASSES = K // (P * PACK)
BLOCKS = M // P
HALF = S // 2
CHUNK = 128
OFF_COLS = HALF // 16


def tile_list_hboth_none_kernel(tc, xT, w_words, w_scales, wgt, wgo, offs, offs2, out):
    nc = tc.nc
    with tc.tile_pool(name="held", bufs=1) as held, tc.psum_pool(name="psum", bufs=1) as psum:
        list_in = held.tile([P, S // 16], U16, name="list_in")
        list_out = held.tile([P, S // 16], U16, name="list_out")
        wgt_sb = held.tile([P, S], F32, name="wgt_sb")
        wgo_sb = held.tile([P, S], F32, name="wgo_sb")
        w_sb = held.tile([P, PASSES, 2 * M], U8, name="w_sb", align_bytes=64)
        wsc = held.tile([P, PASSES, M], U8, name="wsc", align_bytes=64)
        plane = [[held.tile([P, T], F32, name=f"plane{a}_{t}") for t in range(PACK)] for a in range(PASSES)]
        picked = [[held.tile([P, PACK, HALF], F32, name=f"picked{a}_{h}") for h in range(2)] for a in range(PASSES)]
        grouped = [[held.tile([P, HALF, PACK], BF16, name=f"grouped{a}_{h}", align_bytes=64) for h in range(2)] for a in range(PASSES)]
        codes = [[held.tile([P, HALF], U32, name=f"codes{a}_{h}", align_bytes=64) for h in range(2)] for a in range(PASSES)]
        xsc = [[held.tile([P, HALF], U8, name=f"xsc{a}_{h}", align_bytes=64) for h in range(2)] for a in range(PASSES)]
        window = [held.tile([P, T], F32, name=f"window{b}") for b in range(BLOCKS)]
        y_sb = [held.tile([P, S], F32, name=f"y{b}") for b in range(BLOCKS)]
        bank = [psum.tile([P, S], F32, name=f"bank{b}") for b in range(BLOCKS)]

        nc.gpsimd.memset(wsc[:].bitcast(I32), 0)
        for b in range(BLOCKS):
            nc.vector.memset(window[b][:] if b < 4 else window[b][:, 0:8], 0.0)
        for b in range(4, BLOCKS):
            nc.gpsimd.memset(window[b][:], 0.0)

        rows = xT.rearrange("(a p t) n -> a t p n", p=P, t=PACK)
        nc.sync.dma_start(list_in[:], offs)
        nc.sync.dma_start(plane[0][0][:], rows[0, 0])
        nc.scalar.dma_start(wgt_sb[:, 0:HALF], wgt[:, 0:HALF])
        nc.sync.dma_start(wgt_sb[:, HALF:S], wgt[:, HALF:S])
        for a in range(PASSES):
            for t in range(PACK):
                if a + t > 0:
                    nc.sync.dma_start(plane[a][t][:], rows[a, t])
        nc.sync.dma_start(w_sb[:].bitcast(I32), w_words.bitcast(I32).rearrange("a p n -> p a n"))
        for q in range(4):
            nc.sync.dma_start(
                wsc[32 * q : 32 * q + 4].bitcast(I32),
                w_scales.bitcast(I32)[:, 4 * q : 4 * q + 4, :].rearrange("a r n -> r a n"),
            )
        nc.sync.dma_start(list_out[:], offs2)
        nc.sync.dma_start(wgo_sb[:], wgo)

        def gather(a, t, h):
            nc.vector.tensor_tensor(
                picked[a][h][:, t, :],
                plane[a][t][:].indirect(list_in[:, h * OFF_COLS : (h + 1) * OFF_COLS]),
                wgt_sb[:, h * HALF : (h + 1) * HALF],
                MULT,
            )

        def views(a, h, lo, hi):
            return grouped[a][h][:, lo:hi, :], picked[a][h][:, :, lo:hi].rearrange("p t c -> p c t")

        def interleave_scalar(a, h, lo, hi):
            dst, src = views(a, h, lo, hi)
            nc.scalar.copy(dst, src)

        def interleave_vector(a, h, lo, hi):
            dst, src = views(a, h, lo, hi)
            nc.vector.tensor_copy(dst, src)

        def quantize(a, h, lo, hi):
            nc.vector.quantize_mx(
                out=codes[a][h][:, lo:hi].bitcast(FP8X4),
                scales=xsc[a][h][:, lo:hi],
                in_=grouped[a][h][:, lo:hi, :].rearrange("p c t -> p (c t)"),
            )

        def multiply(b, h):
            for c in range(HALF // CHUNK):
                lo = c * CHUNK
                for a in range(PASSES):
                    nc.tensor.matmul_mx(
                        out=bank[b][:, h * HALF + lo : h * HALF + lo + CHUNK],
                        lhsT=w_sb[:, a, 2 * P * b : 2 * P * (b + 1)].bitcast(FP4X4),
                        lhsT_scale=wsc[:, a, P * b : P * (b + 1)],
                        rhs=codes[a][h][:, lo : lo + CHUNK].bitcast(FP8X4),
                        rhs_scale=xsc[a][h][:, lo : lo + CHUNK],
                        start=(a == 0),
                        stop=(a == PASSES - 1),
                    )
            cols = slice(h * HALF, (h + 1) * HALF)
            nc.scalar.copy(y_sb[b][:, cols], bank[b][:, cols])

        def scatter(b, h):
            cols = slice(h * HALF, (h + 1) * HALF)
            nc.vector.tensor_tensor(
                window[b][:].indirect(list_out[:, h * OFF_COLS : (h + 1) * OFF_COLS]),
                y_sb[b][:, cols],
                wgo_sb[:, cols],
                MULT,
            )

        for t in range(PACK):
            gather(0, t, 0)
            gather(0, t, 1)
        interleave_scalar(0, 0, 0, HALF)
        interleave_scalar(0, 1, 0, HALF)
        gather(1, 0, 0)
        gather(1, 0, 1)
        gather(1, 1, 0)
        quantize(0, 0, 0, HALF)
        gather(1, 1, 1)
        gather(1, 2, 0)
        gather(1, 3, 0)
        interleave_scalar(1, 0, 0, CHUNK)
        gather(1, 2, 1)
        interleave_vector(1, 0, CHUNK, HALF)
        quantize(1, 0, 0, CHUNK)
        quantize(1, 0, CHUNK, HALF)
        gather(1, 3, 1)
        quantize(0, 1, 0, HALF)
        for b in range(BLOCKS):
            multiply(b, 0)
            scatter(b, 0)
            if b == 1:
                interleave_scalar(1, 1, 0, HALF)
            if b == 3:
                quantize(1, 1, 0, HALF)
        for b in range(BLOCKS):
            multiply(b, 1)
            scatter(b, 1)
            nc.sync.dma_start(out[P * b : P * (b + 1), :], window[b][:])
